import numpy as np
CORES = [0,1]
N = 2
def setup_inputs(rng):
    return {"x": rng.standard_normal((N, 128, 16384), dtype=np.float32)}
def reference(x):
    g = np.concatenate(list(x), axis=1)
    return {"y": np.broadcast_to(g, (N,) + g.shape)}

COLS = 16384

SCRATCH = {
    "stage": ("sbuf", [128, COLS], "float32"),
    "land": ("sbuf", [128, COLS], "float32"),
}
SEMAPHORES = ["loaded", "read", "arrived", "stored"]


def rank_program(g, core, T, topo):
    rank = T.rank_of(core)
    if rank is None:
        return
    peer_rank = 1 - rank
    peer = T.cores[peer_rank]
    rid, pid = topo.addr(peer)[:2]

    g.dma_start(T.stage[:], T.x[:]).then_inc(T.sem.loaded, 16)
    g.dma_start(T.y[:, rank * COLS:(rank + 1) * COLS], T.x[:]).then_inc(T.sem.stored, 16)

    g.wait_ge(T.sem.loaded, 16)
    g.remote_dma(T.land[:], T.stage[:], T.sem.arrived, T.sem.read, pid, rid, topo.mask(core, peer))

    g.wait_ge(T.sem.arrived, 16)
    g.dma_start(T.y[:, peer_rank * COLS:(peer_rank + 1) * COLS], T.land[:]).then_inc(T.sem.stored, 16)

    g.wait_ge(T.sem.stored, 32)
    g.wait_ge(T.sem.read, 16)
